import numpy as np
import ml_dtypes


def mxq(x, axis, fmt="e4m3"):
    dtype, down = {"e4m3": (ml_dtypes.float8_e4m3fn, 7), "e5m2": (ml_dtypes.float8_e5m2, 14)}[fmt]
    v = np.moveaxis(np.asarray(x, np.float32).astype(ml_dtypes.bfloat16).astype(np.float64), axis, -1)
    blocks = v.reshape(v.shape[:-1] + (-1, 32))
    amax = np.abs(blocks).max(-1, keepdims=True)
    byte = np.maximum(np.where(amax > 0, np.frexp(amax)[1] - 1 + 127, 0) - down, 1)
    scale = np.exp2(byte - 127.0)
    codes = (blocks / scale).astype(np.float32).astype(dtype).astype(np.float64)
    return np.moveaxis((codes * scale).reshape(v.shape), -1, axis)


WIDE = False


def mx_kscale(k):
    if not WIDE:
        return np.ones(k)
    levels = np.array([10, -10, 5, -5, 0])
    if k % 512:
        return np.exp2(np.random.permutation(np.resize(levels, k // 32))).repeat(32)
    a = np.empty((k // 512, 16))
    for p in range(k // 512):
        a[p, :8] = np.random.permutation(np.resize(levels, 8))
        for g in range(8):
            far = levels[np.abs(levels - a[p, g]) >= 10]
            a[p, g + 8] = far[np.random.randint(len(far))]
    return np.exp2(a.ravel()).repeat(32)


def f64(x):
    return np.asarray(x).astype(np.float64)


def striped(idx):
    return np.tile(idx.reshape(-1, 16).T, (8, 1)).astype(np.uint16)


def unstriped(offs):
    return offs[:16].T.reshape(-1).astype(np.int64)


def striped8(idx):
    return np.concatenate([x.reshape(-1, 16).T for x in idx]).astype(np.uint16)


def runs(offs, k):
    lists = np.stack([offs[16 * r : 16 * r + 16].T.reshape(-1) for r in range(8)]).astype(np.int64)
    return lists[np.arange(k) % 512 // 64]


def pack_weight(w):
    k, n = w.shape
    w = f64(np.asarray(w, np.float32).astype(ml_dtypes.bfloat16)).reshape(k // 32, 32, n)
    amax = np.abs(w).max(1)
    byte = np.clip(np.where(amax > 0, np.frexp(amax)[1] - 1 + 127 - 7, 1), 1, 254)
    scaled = (w * np.exp2(127.0 - byte)[:, None, :]).reshape(k, n).astype(np.float32)
    words = np.ascontiguousarray(scaled.reshape(k // 512, 128, 4, n).transpose(0, 1, 3, 2)).astype(ml_dtypes.float8_e4m3fn).view(np.uint8)
    return words, np.ascontiguousarray(byte.astype(np.uint8).reshape(k // 512, 16, n))


def unpack_weight(words, scales):
    g, p, n, _ = words.shape
    vals = np.ascontiguousarray(words).view(ml_dtypes.float8_e4m3fn).astype(np.float64) * np.repeat(np.exp2(scales.astype(np.float64) - 127.0), 8, axis=1)[..., None]
    return vals.transpose(0, 1, 3, 2).reshape(g * 512, n)


E2M1 = np.array([0.0, 0.5, 1.0, 1.5, 2.0, 3.0, 4.0, 6.0, -0.0, -0.5, -1.0, -1.5, -2.0, -3.0, -4.0, -6.0])


def pack_fp4(w):
    k, n = w.shape
    w = f64(np.asarray(w, np.float32).astype(ml_dtypes.bfloat16)).reshape(k // 32, 32, n)
    amax = np.abs(w).max(1)
    mant, ex = np.frexp(amax / 6.0)
    byte = np.clip(np.where(amax > 0, np.where(mant > 0.5, ex, ex - 1) + 127, 1), 1, 254)
    scaled = (w * np.exp2(127.0 - byte)[:, None, :]).reshape(k, n).astype(np.float32)
    c = np.ascontiguousarray(scaled.reshape(k // 512, 128, 4, n).transpose(0, 1, 3, 2)).astype(ml_dtypes.float4_e2m1fn).view(np.uint8) & 0xF
    words = (c[..., 0::2] | (c[..., 1::2] << 4)).reshape(k // 512, 128, 2 * n)
    return np.ascontiguousarray(words), np.ascontiguousarray(byte.astype(np.uint8).reshape(k // 512, 16, n))


def unpack_fp4(words, scales):
    g, _, n = scales.shape
    words = np.ascontiguousarray(words).reshape(g, 128, n, 2)
    nib = np.empty((g, 128, n, 4), np.uint8)
    nib[..., 0::2] = words & 0xF
    nib[..., 1::2] = words >> 4
    vals = E2M1[nib] * np.repeat(np.exp2(scales.astype(np.float64) - 127.0), 8, axis=1)[..., None]
    return vals.transpose(0, 1, 3, 2).reshape(g * 512, n)


def sigmoid(v):
    return 1.0 / (1.0 + np.exp(-np.maximum(v, -700.0)))


K, T, S, N, G, H, W = 512, 2048, 512, 512, 2048, 512, 256


def setup_inputs():
    n = np.random.standard_normal
    s = mx_kscale(K)[:, None]
    u = mx_kscale(S)
    packed_xT = pack_weight(n((K, T)) * s)
    packed_dT = pack_weight(n((K, G)) / s)
    packed_w1 = pack_fp4(n((H, N)) / np.sqrt(2 * H) / u[:, None])
    packed_w2 = pack_fp4(n((K, N)) / np.sqrt(2 * K) / s)
    perm = np.stack([np.random.permutation(S) for _ in range(8)])
    return {
        "x_words": packed_xT[0],
        "x_scales": packed_xT[1],
        "d_words": packed_dT[0],
        "d_scales": packed_dT[1],
        "gn": (np.random.uniform(0.5, 1.5, (H, 1)) * u[:, None]).astype(np.float32),
        "w1_words": packed_w1[0],
        "w1_scales": packed_w1[1],
        "w2_words": packed_w2[0],
        "w2_scales": packed_w2[1],
        "sl": np.random.uniform(1.0, 2.0, (N, 1)).astype(np.float32),
        "th": (0.5 * n((N, 1))).astype(np.float32),
        "offs": striped(np.random.permutation(T)[:S]),
        "k1": striped8(np.random.randint(0, G, (8, H))),
        "n1": striped8(perm[:, :W]),
        "n2": striped8(perm[:, W:]),
        "two": striped(np.random.permutation(T)[:S]),
        "n3": striped8(np.stack([np.random.permutation(S) for _ in range(8)])),
        "n4": striped8(np.stack([np.random.permutation(S) for _ in range(8)])),
    }


def reference(x_words, x_scales, d_words, d_scales, gn, w1_words, w1_scales, w2_words, w2_scales, sl, th, offs, k1, n1, n2, two, n3, n4):
    d_k1 = unpack_weight(d_words, d_scales)[np.arange(K)[:, None], runs(k1, K)]
    xq = unpack_weight(x_words, x_scales)[:, unstriped(offs)]
    s = 0.0625 * (d_k1.T @ xq)
    pa = s[np.arange(H)[:, None], runs(n1, H)]
    pb = s[np.arange(H)[:, None], runs(n2, H)]
    ra = np.maximum(pa, pb)
    ds = s.copy()
    ds[np.arange(H)[:, None], runs(n1, H)] = ra
    z = f64(gn) * ds
    x_two = unpack_weight(x_words, x_scales)[:, unstriped(two)]
    h = unpack_fp4(w1_words, w1_scales).T @ mxq(z, 0, "e4m3") + unpack_fp4(w2_words, w2_scales).T @ x_two
    st = np.maximum(h, h[np.arange(N)[:, None], runs(n3, N)])
    sg = sigmoid(f64(sl) * (st[np.arange(N)[:, None], runs(n4, N)] - f64(th)))
    return st * sg

@@ -1,0 +1,217 @@
+from contextlib import ExitStack
+
+import concourse.mybir as mybir
+
+F32 = mybir.dt.float32
+BF16 = mybir.dt.bfloat16
+I32 = mybir.dt.int32
+U32 = mybir.dt.uint32
+U16 = mybir.dt.uint16
+U8 = mybir.dt.uint8
+FP8X4 = mybir.dt.float8_e4m3fn_x4
+FP4X4 = mybir.dt.float4_e2m1fn_x4
+ALU = mybir.AluOpType
+ACT = mybir.ActivationFunctionType
+
+P = 128
+T = 2048
+S = 512
+HALF = S // 2
+PACK = 4
+FLOPS = 3 * 2 * 512 * 512 * 512
+
+
+def tile_picked_kmixfillehh_none_p_kernel(
+    tc, x_words, x_scales, d_words, d_scales, gn, w1_words, w1_scales, w2_words, w2_scales,
+    sl, th, offs, k1, n1, n2, two, n3, n4, out,
+):
+    nc = tc.nc
+    with ExitStack() as ctx:
+        lists = ctx.enter_context(tc.tile_pool(name="lists", bufs=1))
+        sb = ctx.enter_context(tc.tile_pool(name="sb", bufs=1))
+        psum = ctx.enter_context(tc.psum_pool(name="psum", bufs=1))
+
+        def load_list(src, name):
+            tile = lists.tile(list(src.shape), U16, name=name)
+            nc.sync.dma_start(tile[:], src)
+            return tile
+
+        def load_words(src, name):
+            tile = sb.tile([P, T], U32, name=name, tag=name, align_bytes=64)
+            nc.sync.dma_start(tile[:].bitcast(I32), src[0].rearrange("p n t -> p (n t)").bitcast(I32))
+            return tile
+
+        k1_sb = load_list(k1, "k1_sb")
+        offs_sb = load_list(offs, "offs_sb")
+        n1_sb = load_list(n1, "n1_sb")
+
+        ds_win = sb.tile([P, T], U8, name="ds_win", align_bytes=64)
+        nc.vector.memset(ds_win[:].bitcast(I32), 0)
+        d_rows = d_scales[0].bitcast(I32).rearrange("(g e) c -> e g c", e=2)
+        for e in range(2):
+            nc.sync.dma_start(ds_win[e:P:16, :].bitcast(I32), d_rows[e])
+        d_win = load_words(d_words, "d_win")
+
+        xs_win = sb.tile([P, T], U8, name="xs_win", align_bytes=64)
+        nc.vector.memset(xs_win[:].bitcast(I32), 0)
+        for q in range(4):
+            nc.sync.dma_start(xs_win[32 * q : 32 * q + 4, :].bitcast(I32), x_scales[0, 4 * q : 4 * q + 4, :].bitcast(I32))
+
+        x_win = load_words(x_words, "x_win")
+        two_sb = load_list(two, "two_sb")
+        n2_sb = load_list(n2, "n2_sb")
+        n3_sb = load_list(n3, "n3_sb")
+        n4_sb = load_list(n4, "n4_sb")
+
+        key_bytes = sb.tile([P, S], U8, name="key_bytes", tag="key_bytes", align_bytes=64)
+        nc.vector.tensor_copy(key_bytes[:], ds_win[:].indirect(k1_sb[:]))
+        key_plane = sb.tile([P, S], U8, name="key_plane", align_bytes=64)
+        nc.vector.tensor_copy(
+            key_plane[:].rearrange("p (t m) -> p t m", t=PACK), key_bytes[:].rearrange("p (m t) -> p t m", t=PACK)
+        )
+        for e in range(2):
+            nc.scalar.dma_start(key_plane[2 + e : P : 32, :].bitcast(I32), key_plane[16 + e : P : 32, :].bitcast(I32))
+
+        key_words = sb.tile([P, S], U32, name="key_words", tag="key_words", align_bytes=64)
+        nc.vector.tensor_copy(key_words[:], d_win[:].indirect(k1_sb[:]))
+        key_dealt = sb.tile([P, S], U32, name="key_dealt", align_bytes=64)
+        nc.vector.tensor_copy(
+            key_dealt[:].rearrange("p (t m) -> p m t", t=PACK), key_words[:].rearrange("p (m t) -> p m t", t=PACK)
+        )
+
+        tok_plane = sb.tile([P, S], U8, name="tok_plane", align_bytes=64)
+        nc.vector.tensor_copy(tok_plane[:], xs_win[:].indirect(offs_sb[:]))
+        tok_words = sb.tile([P, S], U32, name="tok_words", align_bytes=64)
+        for j in range(2):
+            nc.vector.tensor_copy(tok_words[:, j * HALF : (j + 1) * HALF], x_win[:].indirect(offs_sb[:, j * 16 : (j + 1) * 16]))
+
+        raw = sb.tile([P, 3, HALF], U32, name="raw", tag="d_win", align_bytes=64)
+        w_raw = raw[:, 0:2, :]
+        ws_raw = raw[:, 2, :].rearrange("p (i c) -> p i c", i=2)
+        for i, src in enumerate((w1_words, w2_words)):
+            nc.sync.dma_start(raw[:, i, :].bitcast(I32), src[0].bitcast(I32))
+        nc.gpsimd.memset(raw[:, 2, :].bitcast(I32), 0)
+        for i, src in enumerate((w1_scales, w2_scales)):
+            for q in range(4):
+                nc.sync.dma_start(
+                    raw[32 * q : 32 * q + 4, 2, i * P : (i + 1) * P].bitcast(I32), src[0, 4 * q : 4 * q + 4, :].bitcast(I32)
+                )
+        rows = sb.tile([P, 3, 8], F32, name="rows", tag="key_words", align_bytes=64)
+        nc.sync.dma_start(rows[:, 0, 0:PACK], gn.rearrange("(p t) o -> p (t o)", t=PACK))
+        with nc.allow_non_contiguous_dma(reason="one value a row"):
+            for i, src in ((1, sl), (2, th)):
+                by_b = src.rearrange("(c t b) o -> b c (t o)", t=PACK, b=4)
+                for b in range(4):
+                    nc.sync.dma_start(rows[b:P:4, i, 0:PACK], by_b[b])
+
+        def score_pass(acc, t, tokens):
+            cols = slice(t * P, (t + 1) * P)
+            nc.tensor.matmul_mx(
+                out=acc, lhsT=key_dealt[:, cols].bitcast(FP8X4), lhsT_scale=key_plane[:, cols],
+                rhs=tok_words[:, tokens].bitcast(FP8X4), rhs_scale=tok_plane[:, tokens], start=True, stop=True,
+            )
+
+        two_plane = sb.tile([P, S], U8, name="two_plane", align_bytes=64)
+        nc.vector.tensor_copy(two_plane[:], xs_win[:].indirect(two_sb[:]))
+        two_words = sb.tile([P, S], U32, name="two_words", align_bytes=64)
+        nc.vector.tensor_copy(two_words[:], x_win[:].indirect(two_sb[:]))
+
+        mixed = []
+        for t in range(PACK):
+            s_sb = sb.tile([P, S], F32, name=f"s_sb{t}")
+            if t == 0:
+                for j, tag in enumerate(("s_first", "s_chain")):
+                    tokens = slice(j * HALF, (j + 1) * HALF)
+                    acc = psum.tile([P, HALF], F32, name="s_half", tag=tag)
+                    score_pass(acc[:], t, tokens)
+                    nc.scalar.activation(s_sb[:, tokens], acc[:], ACT.Copy, scale=0.0625)
+            else:
+                acc = psum.tile([P, S], F32, name="s_acc", tag="s_chain")
+                score_pass(acc[:], t, slice(0, S))
+                nc.scalar.activation(s_sb[:], acc[:], ACT.Copy, scale=0.0625)
+            pa = sb.tile([P, HALF], F32, name="pa", tag=f"pa{t}", align_bytes=64)
+            pb = sb.tile([P, HALF], F32, name="pb", tag=f"pb{t}", align_bytes=64)
+            nc.scalar.activation(pa[:], s_sb[:].indirect(n1_sb[:]), ACT.Copy)
+            nc.scalar.activation(pb[:], s_sb[:].indirect(n2_sb[:]), ACT.Copy)
+            ra = sb.tile([P, HALF], F32, name=f"ra{t}")
+            nc.vector.tensor_tensor(ra[:], pa[:], pb[:], ALU.max)
+            nc.vector.tensor_copy(s_sb[:].indirect(n1_sb[:]), ra[:])
+            mixed.append(s_sb)
+
+        w_dealt = sb.tile([P, 2, HALF], U32, name="w_dealt", align_bytes=64)
+        ws_dealt = sb.tile([P, 2, S // 4], U32, name="ws_dealt", tag="pb3", align_bytes=64)
+        for i in range(2):
+            nc.scalar.copy(
+                w_dealt[:, i, :].rearrange("p (t c u) -> p t c u", t=PACK, u=2),
+                w_raw[:, i, :].rearrange("p (c t u) -> p t c u", t=PACK, u=2),
+            )
+        nc.scalar.copy(
+            ws_dealt[:].rearrange("p i (t c) -> p i t c", t=PACK), ws_raw.rearrange("p i (c t) -> p i t c", t=PACK)
+        )
+        bias = sb.tile([P, PACK], F32, name="bias")
+        nc.vector.scalar_tensor_tensor(bias[:], rows[:, 1, 0:PACK], -1.0, rows[:, 2, 0:PACK], ALU.mult, ALU.mult)
+
+        z_pairs = sb.tile([P, 2, S, 2], BF16, name="z_pairs", tag="pa3", align_bytes=64)
+        for t in range(PACK):
+            if t < 2:
+                nc.scalar.activation(z_pairs[:, t // 2, :, t % 2], mixed[t][:], ACT.Copy, scale=rows[:, 0, t : t + 1])
+            else:
+                nc.vector.tensor_scalar(z_pairs[:, t // 2, :, t % 2], mixed[t][:], rows[:, 0, t : t + 1], None, ALU.mult)
+        z_bf = sb.tile([P, S * PACK], BF16, name="z_bf", align_bytes=64)
+        z_words = sb.tile([P, S], U32, name="z_words", align_bytes=64)
+        z_plane = sb.tile([P, S], U8, name="z_plane", align_bytes=64)
+        pair_words = z_pairs[:].rearrange("p h c e -> p (h c e)").bitcast(I32).rearrange("p (h c) -> p c h", h=2)
+        for j in range(2):
+            cols = slice(j * HALF, (j + 1) * HALF)
+            nc.vector.tensor_copy(
+                z_bf[:].bitcast(I32).rearrange("p (c h) -> p c h", h=2)[:, cols, :], pair_words[:, cols, :]
+            )
+        for j in range(2):
+            cols = slice(j * HALF, (j + 1) * HALF)
+            nc.vector.quantize_mx(
+                out=z_words[:, cols].bitcast(FP8X4), scales=z_plane[:, cols],
+                in_=z_bf[:, j * HALF * PACK : (j + 1) * HALF * PACK],
+            )
+
+        w_bytes = w_dealt[:].rearrange("p i c -> p (i c)").bitcast(U8)
+        ws_bytes = ws_dealt[:].rearrange("p i c -> p (i c)").bitcast(U8)
+        out_rows = out.rearrange("(c t b) j -> t c b j", t=PACK, b=4)
+        halves = [(slice(j * HALF, (j + 1) * HALF), slice(j * 16, (j + 1) * 16)) for j in range(2)]
+        h_acc, h_sb, other, st = [], [], [], []
+        for t in range(PACK):
+            acc = psum.tile([P, S], F32, name=f"h_acc{t}")
+            for step, (i, words, plane) in enumerate(((1, two_words, two_plane), (0, z_words, z_plane))):
+                nc.tensor.matmul_mx(
+                    out=acc[:],
+                    lhsT=w_bytes[:, 2 * (i * S + t * P) : 2 * (i * S + (t + 1) * P)].bitcast(FP4X4),
+                    lhsT_scale=ws_bytes[:, i * S + t * P : i * S + (t + 1) * P],
+                    rhs=words[:].bitcast(FP8X4), rhs_scale=plane[:], start=(step == 0), stop=(step == 1),
+                )
+            h_acc.append(acc)
+            h_sb.append(sb.tile([P, S], F32, name=f"h_sb{t}"))
+            nc.scalar.copy(h_sb[t][:], acc[:])
+        for t in range(PACK):
+            other.append(sb.tile([P, S], F32, name=f"other{t}"))
+            for cols, entries in halves:
+                window = h_sb[t][:].indirect(n3_sb[:, entries])
+                if t == PACK - 1:
+                    nc.scalar.activation(other[t][:, cols], window, ACT.Copy)
+                else:
+                    nc.vector.tensor_copy(other[t][:, cols], window)
+            st.append(sb.tile([P, S], F32, name=f"st{t}"))
+            nc.vector.tensor_tensor(st[t][:], h_acc[t][:], other[t][:], ALU.max)
+        for t in range(PACK):
+            sg = sb.tile([P, S], F32, name=f"sg{t}")
+            res = sb.tile([P, S], F32, name=f"res{t}")
+            for cols, entries in halves:
+                nc.scalar.activation(
+                    sg[:, cols], st[t][:].indirect(n4_sb[:, entries]), ACT.Sigmoid,
+                    bias=bias[:, t : t + 1], scale=rows[:, 1, t : t + 1],
+                )
+            if t < PACK - 1:
+                nc.vector.tensor_tensor(res[:], st[t][:], sg[:], ALU.mult)
+                nc.sync.dma_start(out_rows[t], res[:])
+            else:
+                for cols, entries in halves:
+                    nc.vector.tensor_tensor(res[:, cols], st[t][:, cols], sg[:, cols], ALU.mult)
+                    nc.sync.dma_start(out_rows[t][:, :, cols], res[:, cols])

@@ -76,7 +76,8 @@ def tile_picked_kmixfillehh_none_p_kernel(
         nc.vector.tensor_copy(key_words[:], d_win[:].indirect(k1_sb[:]))
         key_dealt = sb.tile([P, S], U32, name="key_dealt", align_bytes=64)
         nc.vector.tensor_copy(
-            key_dealt[:].rearrange("p (t m) -> p m t", t=PACK), key_words[:].rearrange("p (m t) -> p m t", t=PACK)
+            key_dealt[:].rearrange("p (t c i) -> p c t i", t=PACK, i=4),
+            key_words[:].rearrange("p (c i t) -> p c t i", t=PACK, i=4),
         )
 
         tok_plane = sb.tile([P, S], U8, name="tok_plane", align_bytes=64)
@@ -133,15 +134,15 @@ def tile_picked_kmixfillehh_none_p_kernel(
             pb = sb.tile([P, HALF], F32, name="pb", tag=f"pb{t}", align_bytes=64)
             nc.scalar.activation(pa[:], s_sb[:].indirect(n1_sb[:]), ACT.Copy)
             nc.scalar.activation(pb[:], s_sb[:].indirect(n2_sb[:]), ACT.Copy)
-            ra = sb.tile([P, HALF], F32, name=f"ra{t}")
+            ra = sb.tile([P, HALF], F32, name="ra", tag=f"ra{t}", align_bytes=64)
             nc.vector.tensor_tensor(ra[:], pa[:], pb[:], ALU.max)
             nc.vector.tensor_copy(s_sb[:].indirect(n1_sb[:]), ra[:])
             mixed.append(s_sb)
 
         w_dealt = sb.tile([P, 2, HALF], U32, name="w_dealt", align_bytes=64)
-        ws_dealt = sb.tile([P, 2, S // 4], U32, name="ws_dealt", tag="pb3", align_bytes=64)
+        ws_dealt = sb.tile([P, 2, S // 4], U32, name="ws_dealt", tag="ra2", align_bytes=64)
         for i in range(2):
-            nc.scalar.copy(
+            nc.gpsimd.tensor_copy(
                 w_dealt[:, i, :].rearrange("p (t c u) -> p t c u", t=PACK, u=2),
                 w_raw[:, i, :].rearrange("p (c t u) -> p t c u", t=PACK, u=2),
             )
@@ -151,20 +152,24 @@ def tile_picked_kmixfillehh_none_p_kernel(
         bias = sb.tile([P, PACK], F32, name="bias")
         nc.vector.scalar_tensor_tensor(bias[:], rows[:, 1, 0:PACK], -1.0, rows[:, 2, 0:PACK], ALU.mult, ALU.mult)
 
-        z_pairs = sb.tile([P, 2, S, 2], BF16, name="z_pairs", tag="pa3", align_bytes=64)
+        z_pairs = [
+            sb.tile([P, 2, HALF, 2], BF16, name="z_pairs", tag=tag, align_bytes=64) for tag in ("pa3", "pb3")
+        ]
         for t in range(PACK):
-            if t < 2:
-                nc.scalar.activation(z_pairs[:, t // 2, :, t % 2], mixed[t][:], ACT.Copy, scale=rows[:, 0, t : t + 1])
-            else:
-                nc.vector.tensor_scalar(z_pairs[:, t // 2, :, t % 2], mixed[t][:], rows[:, 0, t : t + 1], None, ALU.mult)
+            for j in range(2):
+                target = z_pairs[j][:, t // 2, :, t % 2]
+                source = mixed[t][:, j * HALF : (j + 1) * HALF]
+                if t < 2:
+                    nc.scalar.activation(target, source, ACT.Copy, scale=rows[:, 0, t : t + 1])
+                else:
+                    nc.vector.tensor_scalar(target, source, rows[:, 0, t : t + 1], None, ALU.mult)
         z_bf = sb.tile([P, S * PACK], BF16, name="z_bf", align_bytes=64)
         z_words = sb.tile([P, S], U32, name="z_words", align_bytes=64)
         z_plane = sb.tile([P, S], U8, name="z_plane", align_bytes=64)
-        pair_words = z_pairs[:].rearrange("p h c e -> p (h c e)").bitcast(I32).rearrange("p (h c) -> p c h", h=2)
         for j in range(2):
-            cols = slice(j * HALF, (j + 1) * HALF)
+            pair_words = z_pairs[j][:].rearrange("p h c e -> p (h c e)").bitcast(I32).rearrange("p (h c) -> p c h", h=2)
             nc.vector.tensor_copy(
-                z_bf[:].bitcast(I32).rearrange("p (c h) -> p c h", h=2)[:, cols, :], pair_words[:, cols, :]
+                z_bf[:, j * HALF * PACK : (j + 1) * HALF * PACK].bitcast(I32).rearrange("p (c h) -> p c h", h=2), pair_words
             )
         for j in range(2):
             cols = slice(j * HALF, (j + 1) * HALF)
@@ -179,17 +184,19 @@ def tile_picked_kmixfillehh_none_p_kernel(
         halves = [(slice(j * HALF, (j + 1) * HALF), slice(j * 16, (j + 1) * 16)) for j in range(2)]
         h_acc, h_sb, other, st = [], [], [], []
         for t in range(PACK):
-            acc = psum.tile([P, S], F32, name=f"h_acc{t}")
-            for step, (i, words, plane) in enumerate(((1, two_words, two_plane), (0, z_words, z_plane))):
-                nc.tensor.matmul_mx(
-                    out=acc[:],
-                    lhsT=w_bytes[:, 2 * (i * S + t * P) : 2 * (i * S + (t + 1) * P)].bitcast(FP4X4),
-                    lhsT_scale=ws_bytes[:, i * S + t * P : i * S + (t + 1) * P],
-                    rhs=words[:].bitcast(FP8X4), rhs_scale=plane[:], start=(step == 0), stop=(step == 1),
-                )
-            h_acc.append(acc)
             h_sb.append(sb.tile([P, S], F32, name=f"h_sb{t}"))
-            nc.scalar.copy(h_sb[t][:], acc[:])
+            pieces = [cols for cols, entries in halves] if t == 0 else [slice(0, S)]
+            for j, cols in enumerate(pieces):
+                acc = psum.tile([P, cols.stop - cols.start], F32, name=f"h_acc{t}{j}")
+                for step, (i, words, plane) in enumerate(((1, two_words, two_plane), (0, z_words, z_plane))):
+                    nc.tensor.matmul_mx(
+                        out=acc[:],
+                        lhsT=w_bytes[:, 2 * (i * S + t * P) : 2 * (i * S + (t + 1) * P)].bitcast(FP4X4),
+                        lhsT_scale=ws_bytes[:, i * S + t * P : i * S + (t + 1) * P],
+                        rhs=words[:, cols].bitcast(FP8X4), rhs_scale=plane[:, cols], start=(step == 0), stop=(step == 1),
+                    )
+                nc.scalar.copy(h_sb[t][:, cols], acc[:])
+            h_acc.append(h_sb[t] if t == 0 else acc)
         for t in range(PACK):
             other.append(sb.tile([P, S], F32, name=f"other{t}"))
             for cols, entries in halves:
@@ -199,19 +206,21 @@ def tile_picked_kmixfillehh_none_p_kernel(
                 else:
                     nc.vector.tensor_copy(other[t][:, cols], window)
             st.append(sb.tile([P, S], F32, name=f"st{t}"))
-            nc.vector.tensor_tensor(st[t][:], h_acc[t][:], other[t][:], ALU.max)
+            for cols, entries in halves:
+                nc.vector.tensor_tensor(st[t][:, cols], h_acc[t][:, cols], other[t][:, cols], ALU.max)
         for t in range(PACK):
             sg = sb.tile([P, S], F32, name=f"sg{t}")
             res = sb.tile([P, S], F32, name=f"res{t}")
-            for cols, entries in halves:
+            last = t == PACK - 1
+            bounds = (0, 256, 384, 512) if last else (0, 256, 512)
+            for lo, hi in zip(bounds, bounds[1:]):
                 nc.scalar.activation(
-                    sg[:, cols], st[t][:].indirect(n4_sb[:, entries]), ACT.Sigmoid,
+                    sg[:, lo:hi], st[t][:].indirect(n4_sb[:, lo // 16 : hi // 16]), ACT.Sigmoid,
                     bias=bias[:, t : t + 1], scale=rows[:, 1, t : t + 1],
                 )
-            if t < PACK - 1:
+                if last:
+                    nc.vector.tensor_tensor(res[:, lo:hi], st[t][:, lo:hi], sg[:, lo:hi], ALU.mult)
+                    nc.sync.dma_start(out_rows[t][:, :, lo:hi], res[:, lo:hi])
+            if not last:
                 nc.vector.tensor_tensor(res[:], st[t][:], sg[:], ALU.mult)
                 nc.sync.dma_start(out_rows[t], res[:])
-            else:
-                for cols, entries in halves:
-                    nc.vector.tensor_tensor(res[:, cols], st[t][:, cols], sg[:, cols], ALU.mult)
-                    nc.sync.dma_start(out_rows[t][:, :, cols], res[:, cols])

@@ -149,7 +149,7 @@ def tile_picked_kmixfillehh_none_p_kernel(
         nc.scalar.copy(
             ws_dealt[:].rearrange("p i (t c) -> p i t c", t=PACK), ws_raw.rearrange("p i (c t) -> p i t c", t=PACK)
         )
-        bias = sb.tile([P, PACK], F32, name="bias")
+        bias = sb.tile([P, PACK], F32, name="bias", tag="ra3", align_bytes=64)
         nc.vector.scalar_tensor_tensor(bias[:], rows[:, 1, 0:PACK], -1.0, rows[:, 2, 0:PACK], ALU.mult, ALU.mult)
 
         z_pairs = [
@@ -184,7 +184,7 @@ def tile_picked_kmixfillehh_none_p_kernel(
         halves = [(slice(j * HALF, (j + 1) * HALF), slice(j * 16, (j + 1) * 16)) for j in range(2)]
         h_acc, h_sb, other, st = [], [], [], []
         for t in range(PACK):
-            h_sb.append(sb.tile([P, S], F32, name=f"h_sb{t}"))
+            h_sb.append(sb.tile([P, S], F32, name="h_sb", tag=f"h_sb{t}"))
             pieces = [cols for cols, entries in halves] if t == 0 else [slice(0, S)]
             for j, cols in enumerate(pieces):
                 acc = psum.tile([P, cols.stop - cols.start], F32, name=f"h_acc{t}{j}")
@@ -195,13 +195,16 @@ def tile_picked_kmixfillehh_none_p_kernel(
                         lhsT_scale=ws_bytes[:, i * S + t * P : i * S + (t + 1) * P],
                         rhs=words[:, cols].bitcast(FP8X4), rhs_scale=plane[:, cols], start=(step == 0), stop=(step == 1),
                     )
-                nc.scalar.copy(h_sb[t][:, cols], acc[:])
+                if j == 0:
+                    nc.scalar.copy(h_sb[t][:, cols], acc[:])
+                else:
+                    nc.vector.tensor_copy(h_sb[t][:, cols], acc[:])
             h_acc.append(h_sb[t] if t == 0 else acc)
         for t in range(PACK):
             other.append(sb.tile([P, S], F32, name=f"other{t}"))
             for cols, entries in halves:
                 window = h_sb[t][:].indirect(n3_sb[:, entries])
-                if t == PACK - 1:
+                if t == 2:
                     nc.scalar.activation(other[t][:, cols], window, ACT.Copy)
                 else:
                     nc.vector.tensor_copy(other[t][:, cols], window)
@@ -209,8 +212,8 @@ def tile_picked_kmixfillehh_none_p_kernel(
             for cols, entries in halves:
                 nc.vector.tensor_tensor(st[t][:, cols], h_acc[t][:, cols], other[t][:, cols], ALU.max)
         for t in range(PACK):
-            sg = sb.tile([P, S], F32, name=f"sg{t}")
-            res = sb.tile([P, S], F32, name=f"res{t}")
+            sg = sb.tile([P, S], F32, name="sg", tag="h_sb2" if t == 0 else f"sg{t}")
+            res = sb.tile([P, S], F32, name="res", tag="h_sb3" if t == 0 else f"res{t}")
             last = t == PACK - 1
             bounds = (0, 256, 384, 512) if last else (0, 256, 512)
             for lo, hi in zip(bounds, bounds[1:]):

@@ -63,6 +63,10 @@ def tile_picked_kmixfillehh_none_p_kernel(
         n3_sb = load_list(n3, "n3_sb")
         n4_sb = load_list(n4, "n4_sb")
 
+        warm = sb.tile([P, 2], F32, name="warm")
+        nc.vector.memset(warm[:, 0:1], 0.0)
+        nc.scalar.activation(warm[:, 1:2], warm[:, 0:1], ACT.Sigmoid)
+
         key_bytes = sb.tile([P, S], U8, name="key_bytes", tag="key_bytes", align_bytes=64)
         nc.vector.tensor_copy(key_bytes[:], ds_win[:].indirect(k1_sb[:]))
         key_plane = sb.tile([P, S], U8, name="key_plane", align_bytes=64)
@@ -149,8 +153,10 @@ def tile_picked_kmixfillehh_none_p_kernel(
         nc.scalar.copy(
             ws_dealt[:].rearrange("p i (t c) -> p i t c", t=PACK), ws_raw.rearrange("p i (c t) -> p i t c", t=PACK)
         )
-        bias = sb.tile([P, PACK], F32, name="bias", tag="ra3", align_bytes=64)
-        nc.vector.scalar_tensor_tensor(bias[:], rows[:, 1, 0:PACK], -1.0, rows[:, 2, 0:PACK], ALU.mult, ALU.mult)
+        bias = sb.tile([P, PACK], F32, name="bias")
+        slope_th = sb.tile([P, PACK], F32, name="slope_th")
+        nc.gpsimd.tensor_tensor(slope_th[:], rows[:, 1, 0:PACK], rows[:, 2, 0:PACK], ALU.mult)
+        nc.gpsimd.tensor_scalar(bias[:], slope_th[:], -1.0, 0.0, ALU.mult, ALU.add)
 
         z_pairs = [
             sb.tile([P, 2, HALF, 2], BF16, name="z_pairs", tag=tag, align_bytes=64) for tag in ("pa3", "pb3")
@@ -195,12 +201,14 @@ def tile_picked_kmixfillehh_none_p_kernel(
                         lhsT_scale=ws_bytes[:, i * S + t * P : i * S + (t + 1) * P],
                         rhs=words[:, cols].bitcast(FP8X4), rhs_scale=plane[:, cols], start=(step == 0), stop=(step == 1),
                     )
-                if j == 0:
-                    nc.scalar.copy(h_sb[t][:, cols], acc[:])
-                else:
+                if j == 1:
                     nc.vector.tensor_copy(h_sb[t][:, cols], acc[:])
+                elif t < PACK - 1:
+                    nc.scalar.copy(h_sb[t][:, cols], acc[:])
             h_acc.append(h_sb[t] if t == 0 else acc)
         for t in range(PACK):
+            if t == PACK - 2:
+                nc.vector.tensor_copy(h_sb[t + 1][:], h_acc[t + 1][:])
             other.append(sb.tile([P, S], F32, name=f"other{t}"))
             for cols, entries in halves:
                 window = h_sb[t][:].indirect(n3_sb[:, entries])
@@ -212,8 +220,8 @@ def tile_picked_kmixfillehh_none_p_kernel(
             for cols, entries in halves:
                 nc.vector.tensor_tensor(st[t][:, cols], h_acc[t][:, cols], other[t][:, cols], ALU.max)
         for t in range(PACK):
-            sg = sb.tile([P, S], F32, name="sg", tag="h_sb2" if t == 0 else f"sg{t}")
-            res = sb.tile([P, S], F32, name="res", tag="h_sb3" if t == 0 else f"res{t}")
+            sg = sb.tile([P, S], F32, name="sg", tag=f"sg{t}")
+            res = sb.tile([P, S], F32, name="res", tag="h_sb3" if t == 1 else f"res{t}")
             last = t == PACK - 1
             bounds = (0, 256, 384, 512) if last else (0, 256, 512)
             for lo, hi in zip(bounds, bounds[1:]):
@@ -225,5 +233,6 @@ def tile_picked_kmixfillehh_none_p_kernel(
                     nc.vector.tensor_tensor(res[:, lo:hi], st[t][:, lo:hi], sg[:, lo:hi], ALU.mult)
                     nc.sync.dma_start(out_rows[t][:, :, lo:hi], res[:, lo:hi])
             if not last:
-                nc.vector.tensor_tensor(res[:], st[t][:], sg[:], ALU.mult)
+                engine = nc.gpsimd if t == 0 else nc.vector
+                engine.tensor_tensor(res[:], st[t][:], sg[:], ALU.mult)
                 nc.sync.dma_start(out_rows[t], res[:])

from contextlib import ExitStack

import concourse.mybir as mybir

F32 = mybir.dt.float32
BF16 = mybir.dt.bfloat16
I32 = mybir.dt.int32
U32 = mybir.dt.uint32
U16 = mybir.dt.uint16
U8 = mybir.dt.uint8
FP8X4 = mybir.dt.float8_e4m3fn_x4
FP4X4 = mybir.dt.float4_e2m1fn_x4
ALU = mybir.AluOpType
ACT = mybir.ActivationFunctionType

P = 128
T = 2048
S = 512
HALF = S // 2
PACK = 4
FLOPS = 3 * 2 * 512 * 512 * 512


def tile_picked_kmixfillehh_none_p_kernel(
    tc, x_words, x_scales, d_words, d_scales, gn, w1_words, w1_scales, w2_words, w2_scales,
    sl, th, offs, k1, n1, n2, two, n3, n4, out,
):
    nc = tc.nc
    with ExitStack() as ctx:
        lists = ctx.enter_context(tc.tile_pool(name="lists", bufs=1))
        sb = ctx.enter_context(tc.tile_pool(name="sb", bufs=1))
        psum = ctx.enter_context(tc.psum_pool(name="psum", bufs=1))

        def load_list(src, name):
            tile = lists.tile(list(src.shape), U16, name=name)
            nc.sync.dma_start(tile[:], src)
            return tile

        def load_words(src, name):
            tile = sb.tile([P, T], U32, name=name, tag=name, align_bytes=64)
            nc.sync.dma_start(tile[:].bitcast(I32), src[0].rearrange("p n t -> p (n t)").bitcast(I32))
            return tile

        k1_sb = load_list(k1, "k1_sb")
        offs_sb = load_list(offs, "offs_sb")
        n1_sb = load_list(n1, "n1_sb")

        ds_win = sb.tile([P, T], U8, name="ds_win", align_bytes=64)
        nc.vector.memset(ds_win[:].bitcast(I32), 0)
        d_rows = d_scales[0].bitcast(I32).rearrange("(g e) c -> e g c", e=2)
        for e in range(2):
            nc.sync.dma_start(ds_win[e:P:16, :].bitcast(I32), d_rows[e])
        d_win = load_words(d_words, "d_win")

        xs_win = sb.tile([P, T], U8, name="xs_win", align_bytes=64)
        nc.vector.memset(xs_win[:].bitcast(I32), 0)
        for q in range(4):
            nc.sync.dma_start(xs_win[32 * q : 32 * q + 4, :].bitcast(I32), x_scales[0, 4 * q : 4 * q + 4, :].bitcast(I32))

        x_win = load_words(x_words, "x_win")
        two_sb = load_list(two, "two_sb")
        n2_sb = load_list(n2, "n2_sb")
        n3_sb = load_list(n3, "n3_sb")
        n4_sb = load_list(n4, "n4_sb")

        warm = sb.tile([P, 2], F32, name="warm")
        nc.vector.memset(warm[:, 0:1], 0.0)
        nc.scalar.activation(warm[:, 1:2], warm[:, 0:1], ACT.Sigmoid)

        key_bytes = sb.tile([P, S], U8, name="key_bytes", tag="key_bytes", align_bytes=64)
        nc.vector.tensor_copy(key_bytes[:], ds_win[:].indirect(k1_sb[:]))
        key_plane = sb.tile([P, S], U8, name="key_plane", align_bytes=64)
        nc.vector.tensor_copy(
            key_plane[:].rearrange("p (t m) -> p t m", t=PACK), key_bytes[:].rearrange("p (m t) -> p t m", t=PACK)
        )
        for e in range(2):
            nc.scalar.dma_start(key_plane[2 + e : P : 32, :].bitcast(I32), key_plane[16 + e : P : 32, :].bitcast(I32))

        key_words = sb.tile([P, S], U32, name="key_words", tag="key_words", align_bytes=64)
        nc.vector.tensor_copy(key_words[:], d_win[:].indirect(k1_sb[:]))
        key_dealt = sb.tile([P, S], U32, name="key_dealt", align_bytes=64)
        nc.vector.tensor_copy(
            key_dealt[:].rearrange("p (t c i) -> p c t i", t=PACK, i=4),
            key_words[:].rearrange("p (c i t) -> p c t i", t=PACK, i=4),
        )

        tok_plane = sb.tile([P, S], U8, name="tok_plane", align_bytes=64)
        nc.vector.tensor_copy(tok_plane[:], xs_win[:].indirect(offs_sb[:]))
        tok_words = sb.tile([P, S], U32, name="tok_words", align_bytes=64)
        for j in range(2):
            nc.vector.tensor_copy(tok_words[:, j * HALF : (j + 1) * HALF], x_win[:].indirect(offs_sb[:, j * 16 : (j + 1) * 16]))

        raw = sb.tile([P, 3, HALF], U32, name="raw", tag="d_win", align_bytes=64)
        w_raw = raw[:, 0:2, :]
        ws_raw = raw[:, 2, :].rearrange("p (i c) -> p i c", i=2)
        for i, src in enumerate((w1_words, w2_words)):
            nc.sync.dma_start(raw[:, i, :].bitcast(I32), src[0].bitcast(I32))
        nc.gpsimd.memset(raw[:, 2, :].bitcast(I32), 0)
        for i, src in enumerate((w1_scales, w2_scales)):
            for q in range(4):
                nc.sync.dma_start(
                    raw[32 * q : 32 * q + 4, 2, i * P : (i + 1) * P].bitcast(I32), src[0, 4 * q : 4 * q + 4, :].bitcast(I32)
                )
        rows = sb.tile([P, 3, 8], F32, name="rows", tag="key_words", align_bytes=64)
        nc.sync.dma_start(rows[:, 0, 0:PACK], gn.rearrange("(p t) o -> p (t o)", t=PACK))
        with nc.allow_non_contiguous_dma(reason="one value a row"):
            for i, src in ((1, sl), (2, th)):
                by_b = src.rearrange("(c t b) o -> b c (t o)", t=PACK, b=4)
                for b in range(4):
                    nc.sync.dma_start(rows[b:P:4, i, 0:PACK], by_b[b])

        def score_pass(acc, t, tokens):
            cols = slice(t * P, (t + 1) * P)
            nc.tensor.matmul_mx(
                out=acc, lhsT=key_dealt[:, cols].bitcast(FP8X4), lhsT_scale=key_plane[:, cols],
                rhs=tok_words[:, tokens].bitcast(FP8X4), rhs_scale=tok_plane[:, tokens], start=True, stop=True,
            )

        two_plane = sb.tile([P, S], U8, name="two_plane", align_bytes=64)
        nc.vector.tensor_copy(two_plane[:], xs_win[:].indirect(two_sb[:]))
        two_words = sb.tile([P, S], U32, name="two_words", align_bytes=64)
        nc.vector.tensor_copy(two_words[:], x_win[:].indirect(two_sb[:]))

        mixed = []
        for t in range(PACK):
            s_sb = sb.tile([P, S], F32, name=f"s_sb{t}")
            if t == 0:
                for j, tag in enumerate(("s_first", "s_chain")):
                    tokens = slice(j * HALF, (j + 1) * HALF)
                    acc = psum.tile([P, HALF], F32, name="s_half", tag=tag)
                    score_pass(acc[:], t, tokens)
                    nc.scalar.activation(s_sb[:, tokens], acc[:], ACT.Copy, scale=0.0625)
            else:
                acc = psum.tile([P, S], F32, name="s_acc", tag="s_chain")
                score_pass(acc[:], t, slice(0, S))
                nc.scalar.activation(s_sb[:], acc[:], ACT.Copy, scale=0.0625)
            pa = sb.tile([P, HALF], F32, name="pa", tag=f"pa{t}", align_bytes=64)
            pb = sb.tile([P, HALF], F32, name="pb", tag=f"pb{t}", align_bytes=64)
            nc.scalar.activation(pa[:], s_sb[:].indirect(n1_sb[:]), ACT.Copy)
            nc.scalar.activation(pb[:], s_sb[:].indirect(n2_sb[:]), ACT.Copy)
            ra = sb.tile([P, HALF], F32, name="ra", tag=f"ra{t}", align_bytes=64)
            nc.vector.tensor_tensor(ra[:], pa[:], pb[:], ALU.max)
            nc.vector.tensor_copy(s_sb[:].indirect(n1_sb[:]), ra[:])
            mixed.append(s_sb)

        w_dealt = sb.tile([P, 2, HALF], U32, name="w_dealt", align_bytes=64)
        ws_dealt = sb.tile([P, 2, S // 4], U32, name="ws_dealt", tag="ra2", align_bytes=64)
        for i in range(2):
            nc.gpsimd.tensor_copy(
                w_dealt[:, i, :].rearrange("p (t c u) -> p t c u", t=PACK, u=2),
                w_raw[:, i, :].rearrange("p (c t u) -> p t c u", t=PACK, u=2),
            )
        nc.scalar.copy(
            ws_dealt[:].rearrange("p i (t c) -> p i t c", t=PACK), ws_raw.rearrange("p i (c t) -> p i t c", t=PACK)
        )
        bias = sb.tile([P, PACK], F32, name="bias")
        slope_th = sb.tile([P, PACK], F32, name="slope_th")
        nc.gpsimd.tensor_tensor(slope_th[:], rows[:, 1, 0:PACK], rows[:, 2, 0:PACK], ALU.mult)
        nc.gpsimd.tensor_scalar(bias[:], slope_th[:], -1.0, 0.0, ALU.mult, ALU.add)

        z_pairs = [
            sb.tile([P, 2, HALF, 2], BF16, name="z_pairs", tag=tag, align_bytes=64) for tag in ("pa3", "pb3")
        ]
        for t in range(PACK):
            for j in range(2):
                target = z_pairs[j][:, t // 2, :, t % 2]
                source = mixed[t][:, j * HALF : (j + 1) * HALF]
                if t < 2:
                    nc.scalar.activation(target, source, ACT.Copy, scale=rows[:, 0, t : t + 1])
                else:
                    nc.vector.tensor_scalar(target, source, rows[:, 0, t : t + 1], None, ALU.mult)
        z_bf = sb.tile([P, S * PACK], BF16, name="z_bf", align_bytes=64)
        z_words = sb.tile([P, S], U32, name="z_words", align_bytes=64)
        z_plane = sb.tile([P, S], U8, name="z_plane", align_bytes=64)
        for j in range(2):
            pair_words = z_pairs[j][:].rearrange("p h c e -> p (h c e)").bitcast(I32).rearrange("p (h c) -> p c h", h=2)
            nc.vector.tensor_copy(
                z_bf[:, j * HALF * PACK : (j + 1) * HALF * PACK].bitcast(I32).rearrange("p (c h) -> p c h", h=2), pair_words
            )
        for j in range(2):
            cols = slice(j * HALF, (j + 1) * HALF)
            nc.vector.quantize_mx(
                out=z_words[:, cols].bitcast(FP8X4), scales=z_plane[:, cols],
                in_=z_bf[:, j * HALF * PACK : (j + 1) * HALF * PACK],
            )

        w_bytes = w_dealt[:].rearrange("p i c -> p (i c)").bitcast(U8)
        ws_bytes = ws_dealt[:].rearrange("p i c -> p (i c)").bitcast(U8)
        out_rows = out.rearrange("(c t b) j -> t c b j", t=PACK, b=4)
        halves = [(slice(j * HALF, (j + 1) * HALF), slice(j * 16, (j + 1) * 16)) for j in range(2)]
        h_acc, h_sb, other, st = [], [], [], []
        for t in range(PACK):
            h_sb.append(sb.tile([P, S], F32, name="h_sb", tag=f"h_sb{t}"))
            pieces = [cols for cols, entries in halves] if t == 0 else [slice(0, S)]
            for j, cols in enumerate(pieces):
                acc = psum.tile([P, cols.stop - cols.start], F32, name=f"h_acc{t}{j}")
                for step, (i, words, plane) in enumerate(((1, two_words, two_plane), (0, z_words, z_plane))):
                    nc.tensor.matmul_mx(
                        out=acc[:],
                        lhsT=w_bytes[:, 2 * (i * S + t * P) : 2 * (i * S + (t + 1) * P)].bitcast(FP4X4),
                        lhsT_scale=ws_bytes[:, i * S + t * P : i * S + (t + 1) * P],
                        rhs=words[:, cols].bitcast(FP8X4), rhs_scale=plane[:, cols], start=(step == 0), stop=(step == 1),
                    )
                if j == 1:
                    nc.vector.tensor_copy(h_sb[t][:, cols], acc[:])
                elif t < PACK - 1:
                    nc.scalar.copy(h_sb[t][:, cols], acc[:])
            h_acc.append(h_sb[t] if t == 0 else acc)
        for t in range(PACK):
            if t == PACK - 2:
                nc.vector.tensor_copy(h_sb[t + 1][:], h_acc[t + 1][:])
            other.append(sb.tile([P, S], F32, name=f"other{t}"))
            for cols, entries in halves:
                window = h_sb[t][:].indirect(n3_sb[:, entries])
                if t == 2:
                    nc.scalar.activation(other[t][:, cols], window, ACT.Copy)
                else:
                    nc.vector.tensor_copy(other[t][:, cols], window)
            st.append(sb.tile([P, S], F32, name=f"st{t}"))
            for cols, entries in halves:
                nc.vector.tensor_tensor(st[t][:, cols], h_acc[t][:, cols], other[t][:, cols], ALU.max)
        for t in range(PACK):
            sg = sb.tile([P, S], F32, name="sg", tag=f"sg{t}")
            res = sb.tile([P, S], F32, name="res", tag="h_sb3" if t == 1 else f"res{t}")
            last = t == PACK - 1
            bounds = (0, 256, 384, 512) if last else (0, 256, 512)
            for lo, hi in zip(bounds, bounds[1:]):
                nc.scalar.activation(
                    sg[:, lo:hi], st[t][:].indirect(n4_sb[:, lo // 16 : hi // 16]), ACT.Sigmoid,
                    bias=bias[:, t : t + 1], scale=rows[:, 1, t : t + 1],
                )
                if last:
                    nc.vector.tensor_tensor(res[:, lo:hi], st[t][:, lo:hi], sg[:, lo:hi], ALU.mult)
                    nc.sync.dma_start(out_rows[t][:, :, lo:hi], res[:, lo:hi])
            if not last:
                engine = nc.gpsimd if t == 0 else nc.vector
                engine.tensor_tensor(res[:], st[t][:], sg[:], ALU.mult)
                nc.sync.dma_start(out_rows[t], res[:])
